import numpy as np
import ml_dtypes


def mxq(x, axis, fmt="e4m3"):
    dtype, down = {"e4m3": (ml_dtypes.float8_e4m3fn, 7), "e5m2": (ml_dtypes.float8_e5m2, 14)}[fmt]
    v = np.moveaxis(np.asarray(x, np.float32).astype(ml_dtypes.bfloat16).astype(np.float64), axis, -1)
    blocks = v.reshape(v.shape[:-1] + (-1, 32))
    amax = np.abs(blocks).max(-1, keepdims=True)
    byte = np.maximum(np.where(amax > 0, np.frexp(amax)[1] - 1 + 127, 0) - down, 1)
    scale = np.exp2(byte - 127.0)
    codes = (blocks / scale).astype(np.float32).astype(dtype).astype(np.float64)
    return np.moveaxis((codes * scale).reshape(v.shape), -1, axis)


WIDE = False


def mx_kscale(k):
    if not WIDE:
        return np.ones(k)
    levels = np.array([10, -10, 5, -5, 0])
    if k % 512:
        return np.exp2(np.random.permutation(np.resize(levels, k // 32))).repeat(32)
    a = np.empty((k // 512, 16))
    for p in range(k // 512):
        a[p, :8] = np.random.permutation(np.resize(levels, 8))
        for g in range(8):
            far = levels[np.abs(levels - a[p, g]) >= 10]
            a[p, g + 8] = far[np.random.randint(len(far))]
    return np.exp2(a.ravel()).repeat(32)


def f64(x):
    return np.asarray(x).astype(np.float64)


E2M1 = np.array([0.0, 0.5, 1.0, 1.5, 2.0, 3.0, 4.0, 6.0, -0.0, -0.5, -1.0, -1.5, -2.0, -3.0, -4.0, -6.0])


def pack_weight(w, fmt):
    k, n = w.shape
    w = f64(np.asarray(w, np.float32).astype(ml_dtypes.bfloat16)).reshape(k // 32, 32, n)
    amax = np.abs(w).max(1)
    if fmt == "e4m3":
        byte = np.frexp(amax)[1] - 1 + 127 - 7
    else:
        mant, ex = np.frexp(amax / 6.0)
        byte = np.where(mant > 0.5, ex, ex - 1) + 127
    byte = np.clip(np.where(amax > 0, byte, 1), 1, 254)
    scaled = (w * np.exp2(127.0 - byte)[:, None, :]).reshape(k, n).astype(np.float32)
    by_word = np.ascontiguousarray(scaled.reshape(k // 512, 128, 4, n).transpose(0, 1, 3, 2))
    if fmt == "e4m3":
        words = by_word.astype(ml_dtypes.float8_e4m3fn).view(np.uint8)
    else:
        c = by_word.astype(ml_dtypes.float4_e2m1fn).view(np.uint8) & 0xF
        words = (c[..., 0::2] | (c[..., 1::2] << 4)).reshape(k // 512, 128, 2 * n)
    return np.ascontiguousarray(words), np.ascontiguousarray(byte.astype(np.uint8).reshape(k // 512, 16, n))


def unpack_weight(words, scales, fmt):
    g, _, n = scales.shape
    words = np.ascontiguousarray(words).reshape(g, 128, n, -1)
    if fmt == "e4m3":
        vals = words.view(ml_dtypes.float8_e4m3fn).astype(np.float64)
    else:
        nib = np.empty((g, 128, n, 4), np.uint8)
        nib[..., 0::2] = words & 0xF
        nib[..., 1::2] = words >> 4
        vals = E2M1[nib]
    vals = vals * np.repeat(np.exp2(scales.astype(np.float64) - 127.0), 8, axis=1)[..., None]
    return vals.transpose(0, 1, 3, 2).reshape(g * 512, n)


def silu(v):
    return v / (1.0 + np.exp(-np.maximum(v, -700.0)))


K, M, T = 2048, 512, 1536


def setup_inputs():
    n = np.random.standard_normal
    s = mx_kscale(K)[:, None]
    p_w4 = pack_weight(n((K, M)) / np.sqrt(K) / s, "e2m1")
    p_w8 = pack_weight(n((K, M)) / np.sqrt(K) / s, "e4m3")
    return {
        "x": (n((K, T)) * s).astype(np.float32),
        "w4_words": p_w4[0],
        "w4_scales": p_w4[1],
        "w8_words": p_w8[0],
        "w8_scales": p_w8[1],
        "r": (n((1536, 512))).astype(np.float32),
    }


def reference(x, w4_words, w4_scales, w8_words, w8_scales, r):
    x_ = mxq(f64(x), 0, "e4m3")
    w4_ = unpack_weight(w4_words, w4_scales, "e2m1")
    w8_ = unpack_weight(w8_words, w8_scales, "e4m3")
    y = x_.T @ w4_
    u = x_.T @ w8_
    y = silu(y) * u
    return f64(r) + y

@@ -1,0 +1,191 @@
+from contextlib import ExitStack
+
+import concourse.mybir as mybir
+
+K, N, T = 2048, 512, 1536
+FLOPS = 2 * 2 * K * N * T
+
+F32 = mybir.dt.float32
+BF16 = mybir.dt.bfloat16
+I32 = mybir.dt.int32
+U32 = mybir.dt.uint32
+U8 = mybir.dt.uint8
+FP8X4 = mybir.dt.float8_e4m3fn_x4
+FP4X4 = mybir.dt.float4_e2m1fn_x4
+ACT = mybir.ActivationFunctionType
+ALU = mybir.AluOpType
+
+P = 128
+PACK = 4
+PASSES = K // (P * PACK)
+TILES = 4
+GROUP = P * TILES
+GROUPS = T // GROUP
+VECTOR_ROWS = 72
+
+
+def tile_mix_glu48_tm_res_kernel(tc, x, w4_words, w4_scales, w8_words, w8_scales, r, out):
+    nc = tc.nc
+    x_view = x.rearrange("(a p j) t -> a p j t", p=P, j=PACK)
+    r_view = r.rearrange("(g m i) n -> g m i n", m=P, i=TILES)
+    out_view = out.rearrange("(g m i) n -> g m i n", m=P, i=TILES)
+
+    with ExitStack() as ctx:
+        keep = ctx.enter_context(tc.tile_pool(name="keep", bufs=1))
+        raw = ctx.enter_context(tc.tile_pool(name="raw", bufs=PASSES * GROUPS - 2))
+        stage = ctx.enter_context(tc.tile_pool(name="stage", bufs=4))
+        quant = ctx.enter_context(tc.tile_pool(name="quant", bufs=PASSES * GROUPS))
+        ends = ctx.enter_context(tc.tile_pool(name="ends", bufs=GROUPS))
+        psum = ctx.enter_context(tc.psum_pool(name="psum", bufs=1))
+        ctx.enter_context(tc.manual_schedule())
+
+        warm = keep.tile([P, 1], F32, name="warm")
+        warm_out = keep.tile([P, 1], F32, name="warm_out")
+        nc.vector.memset(warm[:], 0.0)
+        nc.scalar.activation(out=warm_out[:], in_=warm[:], func=ACT.Silu)
+
+        s4 = keep.tile([P, PASSES, N], U8, name="s4", align_bytes=64)
+        s8 = keep.tile([P, N], U8, name="s8", align_bytes=64)
+        nc.vector.memset(s4[:].rearrange("p a n -> p (a n)").bitcast(I32), 0)
+        nc.vector.memset(s8[:].bitcast(I32), 0)
+
+        for q in range(4):
+            nc.scalar.dma_start(
+                out=s4[32 * q : 32 * q + 4, :, :].bitcast(I32),
+                in_=w4_scales.rearrange("a q n -> q a n")[4 * q : 4 * q + 4].bitcast(I32),
+            )
+        raw_tiles = {}
+
+        def load_x(a, g):
+            t = raw.tile([P, PACK, GROUP], F32, name="rawx", align_bytes=64)
+            nc.sync.dma_start(out=t[:], in_=x_view[a][:, :, g * GROUP : (g + 1) * GROUP])
+            raw_tiles[a, g] = t[:]
+
+        load_x(0, 0)
+        def load_s8(q):
+            nc.scalar.dma_start(
+                out=s8[32 * q : 32 * q + 16, :].bitcast(I32),
+                in_=w8_scales[:, 4 * q : 4 * q + 4, :].bitcast(I32),
+            )
+
+        for q in range(3):
+            load_s8(q)
+        w8 = keep.tile([P, PASSES, N], U32, name="w8", align_bytes=64)
+        nc.sync.dma_start(out=w8[:].bitcast(I32), in_=w8_words.rearrange("a p n t -> p a (n t)").bitcast(I32))
+        load_s8(3)
+        w4 = keep.tile([P, PASSES, 2 * N], U8, name="w4", align_bytes=64)
+        nc.sync.dma_start(out=w4[:].bitcast(I32), in_=w4_words.rearrange("a p n -> p a n").bitcast(I32))
+
+        r_tiles = {}
+
+        def load_r(g):
+            t = ends.tile([P, TILES, N], F32, name="res")
+            nc.sync.dma_start(out=t[:], in_=r_view[g])
+            r_tiles[g] = t
+
+        for a in range(1, PASSES):
+            load_x(a, 0)
+        x0 = keep.tile([P, PACK, 2 * GROUP], F32, name="x0", align_bytes=64)
+        nc.sync.dma_start(out=x0[:], in_=x_view[0][:, :, GROUP:])
+        raw_tiles[0, 1] = x0[:, :, :GROUP]
+        raw_tiles[0, 2] = x0[:, :, GROUP:]
+        for a in range(1, PASSES):
+            load_x(a, 1)
+        load_r(0)
+        for a in range(1, PASSES):
+            load_x(a, 2)
+        load_r(1)
+        load_r(2)
+
+        codes = {}
+        scales = {}
+
+        def prepare(a, g):
+            grouped = stage.tile([P, TILES, P, PACK], BF16, name="grouped", align_bytes=64)
+            src = raw_tiles[a, g].rearrange("p j (m i) -> p m j i", i=TILES)
+            dst = grouped[:].rearrange("p i m j -> p m j i")
+            nc.scalar.copy(out=dst[:, VECTOR_ROWS:], in_=src[:, VECTOR_ROWS:])
+            nc.vector.tensor_copy(out=dst[:, :VECTOR_ROWS], in_=src[:, :VECTOR_ROWS])
+            c = quant.tile([P, GROUP], U32, name="codes", align_bytes=64)
+            s = quant.tile([P, GROUP], U8, name="scales", align_bytes=64)
+            nc.vector.quantize_mx(
+                out=c[:].bitcast(FP8X4), scales=s[:], in_=grouped[:].rearrange("p i m j -> p (i m j)")
+            )
+            codes[a, g] = c
+            scales[a, g] = s
+
+        gate = {}
+        up = {}
+
+        def multiply(a, g, tiles=range(TILES)):
+            for i in tiles:
+                if a == 0:
+                    gate[g, i] = psum.tile([P, N], F32, name="gate%d" % i)
+                    up[g, i] = psum.tile([P, N], F32, name="up%d" % i)
+                cols = slice(i * P, (i + 1) * P)
+                lhs = codes[a, g][:, cols].bitcast(FP8X4)
+                lhs_scale = scales[a, g][:, cols]
+                flags = dict(start=(a == 0), stop=(a == PASSES - 1))
+                nc.tensor.matmul_mx(
+                    out=gate[g, i][:], lhsT=lhs, lhsT_scale=lhs_scale,
+                    rhs=w4[:, a, :].bitcast(FP4X4), rhs_scale=s4[:, a, :], **flags,
+                )
+                w8_scale = s8[4 * a :, :]
+                nc.tensor.matmul_mx(
+                    out=up[g, i][:], lhsT=lhs, lhsT_scale=lhs_scale,
+                    rhs=w8[:, a, :].bitcast(FP8X4), rhs_scale=w8_scale, **flags,
+                )
+
+        y_tiles = {}
+
+        def finish(g, i):
+            if i == 0:
+                y_tiles[g] = ends.tile([P, TILES, N], F32, name="y")
+            s = stage.tile([P, N], F32, name="silu")
+            nc.scalar.activation(out=s[:], in_=gate[g, i][:], func=ACT.Silu)
+            nc.vector.tensor_tensor(out=y_tiles[g][:, i, :], in0=s[:], in1=up[g, i][:], op=ALU.mult)
+
+        def add(g, i0, i1):
+            y = y_tiles[g]
+            nc.vector.tensor_tensor(
+                out=y[:, i0:i1, :], in0=y[:, i0:i1, :], in1=r_tiles[g][:, i0:i1, :], op=ALU.add
+            )
+
+        def store(g, i0, i1):
+            nc.sync.dma_start(out=out_view[g][:, i0:i1, :], in_=y_tiles[g][:, i0:i1, :])
+
+        for a in range(PASSES):
+            prepare(a, 0)
+            multiply(a, 0)
+        prepare(0, 1)
+        for i in range(TILES):
+            finish(0, i)
+        multiply(0, 1)
+        prepare(1, 1)
+        multiply(1, 1)
+        prepare(2, 1)
+        multiply(2, 1)
+        prepare(0, 2)
+        prepare(3, 1)
+        multiply(3, 1)
+        prepare(1, 2)
+        for i in range(TILES):
+            finish(1, i)
+        multiply(0, 2)
+        multiply(1, 2)
+        add(0, 0, 2)
+        add(0, 2, 4)
+        prepare(2, 2)
+        store(0, 0, 4)
+        prepare(3, 2)
+        for i in range(TILES):
+            multiply(2, 2, [i])
+            multiply(3, 2, [i])
+        add(1, 0, 2)
+        add(1, 2, 4)
+        store(1, 0, 4)
+        for i in range(TILES):
+            finish(2, i)
+            add(2, i, i + 1)
+            if i % 2 == 1:
+                store(2, i - 1, i + 1)

@@ -21,7 +21,7 @@ PASSES = K // (P * PACK)
 TILES = 4
 GROUP = P * TILES
 GROUPS = T // GROUP
-VECTOR_ROWS = 72
+VECTOR_ROWS = (80, 64, 56)
 
 
 def tile_mix_glu48_tm_res_kernel(tc, x, w4_words, w4_scales, w8_words, w8_scales, r, out):
@@ -38,11 +38,6 @@ def tile_mix_glu48_tm_res_kernel(tc, x, w4_words, w4_scales, w8_words, w8_scales
         ends = ctx.enter_context(tc.tile_pool(name="ends", bufs=GROUPS))
         psum = ctx.enter_context(tc.psum_pool(name="psum", bufs=1))
         ctx.enter_context(tc.manual_schedule())
-
-        warm = keep.tile([P, 1], F32, name="warm")
-        warm_out = keep.tile([P, 1], F32, name="warm_out")
-        nc.vector.memset(warm[:], 0.0)
-        nc.scalar.activation(out=warm_out[:], in_=warm[:], func=ACT.Silu)
 
         s4 = keep.tile([P, PASSES, N], U8, name="s4", align_bytes=64)
         s8 = keep.tile([P, N], U8, name="s8", align_bytes=64)
@@ -68,11 +63,8 @@ def tile_mix_glu48_tm_res_kernel(tc, x, w4_words, w4_scales, w8_words, w8_scales
                 in_=w8_scales[:, 4 * q : 4 * q + 4, :].bitcast(I32),
             )
 
-        for q in range(3):
-            load_s8(q)
         w8 = keep.tile([P, PASSES, N], U32, name="w8", align_bytes=64)
         nc.sync.dma_start(out=w8[:].bitcast(I32), in_=w8_words.rearrange("a p n t -> p a (n t)").bitcast(I32))
-        load_s8(3)
         w4 = keep.tile([P, PASSES, 2 * N], U8, name="w4", align_bytes=64)
         nc.sync.dma_start(out=w4[:].bitcast(I32), in_=w4_words.rearrange("a p n -> p a n").bitcast(I32))
 
@@ -83,7 +75,14 @@ def tile_mix_glu48_tm_res_kernel(tc, x, w4_words, w4_scales, w8_words, w8_scales
             nc.sync.dma_start(out=t[:], in_=r_view[g])
             r_tiles[g] = t
 
-        for a in range(1, PASSES):
+        load_x(1, 0)
+        for q in range(4):
+            load_s8(q)
+        warm = keep.tile([P, 1], F32, name="warm")
+        warm_out = keep.tile([P, 1], F32, name="warm_out")
+        nc.vector.memset(warm[:], 0.0)
+        nc.scalar.activation(out=warm_out[:], in_=warm[:], func=ACT.Silu)
+        for a in range(2, PASSES):
             load_x(a, 0)
         x0 = keep.tile([P, PACK, 2 * GROUP], F32, name="x0", align_bytes=64)
         nc.sync.dma_start(out=x0[:], in_=x_view[0][:, :, GROUP:])
@@ -104,8 +103,9 @@ def tile_mix_glu48_tm_res_kernel(tc, x, w4_words, w4_scales, w8_words, w8_scales
             grouped = stage.tile([P, TILES, P, PACK], BF16, name="grouped", align_bytes=64)
             src = raw_tiles[a, g].rearrange("p j (m i) -> p m j i", i=TILES)
             dst = grouped[:].rearrange("p i m j -> p m j i")
-            nc.scalar.copy(out=dst[:, VECTOR_ROWS:], in_=src[:, VECTOR_ROWS:])
-            nc.vector.tensor_copy(out=dst[:, :VECTOR_ROWS], in_=src[:, :VECTOR_ROWS])
+            mv = VECTOR_ROWS[g]
+            nc.scalar.copy(out=dst[:, mv:], in_=src[:, mv:])
+            nc.vector.tensor_copy(out=dst[:, :mv], in_=src[:, :mv])
             c = quant.tile([P, GROUP], U32, name="codes", align_bytes=64)
             s = quant.tile([P, GROUP], U8, name="scales", align_bytes=64)
             nc.vector.quantize_mx(
@@ -157,35 +157,44 @@ def tile_mix_glu48_tm_res_kernel(tc, x, w4_words, w4_scales, w8_words, w8_scales
         for a in range(PASSES):
             prepare(a, 0)
             multiply(a, 0)
-        prepare(0, 1)
         for i in range(TILES):
             finish(0, i)
+        prepare(0, 1)
         multiply(0, 1)
+        prepare(0, 2)
         prepare(1, 1)
         multiply(1, 1)
         prepare(2, 1)
-        multiply(2, 1)
-        prepare(0, 2)
         prepare(3, 1)
-        multiply(3, 1)
-        prepare(1, 2)
         for i in range(TILES):
-            finish(1, i)
-        multiply(0, 2)
-        multiply(1, 2)
+            multiply(2, 1, [i])
+            multiply(3, 1, [i])
         add(0, 0, 2)
         add(0, 2, 4)
-        prepare(2, 2)
         store(0, 0, 4)
+        finish(1, 0)
+        finish(1, 1)
+        prepare(1, 2)
+        finish(1, 2)
+        finish(1, 3)
+        multiply(0, 2)
+        multiply(1, 2)
+        prepare(2, 2)
         prepare(3, 2)
         for i in range(TILES):
             multiply(2, 2, [i])
             multiply(3, 2, [i])
         add(1, 0, 2)
+        store(1, 0, 2)
         add(1, 2, 4)
-        store(1, 0, 4)
-        for i in range(TILES):
-            finish(2, i)
-            add(2, i, i + 1)
-            if i % 2 == 1:
-                store(2, i - 1, i + 1)
+        store(1, 2, 4)
+        finish(2, 0)
+        finish(2, 1)
+        add(2, 0, 1)
+        finish(2, 2)
+        add(2, 1, 2)
+        store(2, 0, 2)
+        finish(2, 3)
+        add(2, 2, 3)
+        add(2, 3, 4)
+        store(2, 2, 4)

@@ -21,7 +21,7 @@ PASSES = K // (P * PACK)
 TILES = 4
 GROUP = P * TILES
 GROUPS = T // GROUP
-VECTOR_ROWS = (80, 64, 56)
+VECTOR_ROWS = (88, 64, 56)
 
 
 def tile_mix_glu48_tm_res_kernel(tc, x, w4_words, w4_scales, w8_words, w8_scales, r, out):
@@ -32,7 +32,7 @@ def tile_mix_glu48_tm_res_kernel(tc, x, w4_words, w4_scales, w8_words, w8_scales
 
     with ExitStack() as ctx:
         keep = ctx.enter_context(tc.tile_pool(name="keep", bufs=1))
-        raw = ctx.enter_context(tc.tile_pool(name="raw", bufs=PASSES * GROUPS - 2))
+        raw = ctx.enter_context(tc.tile_pool(name="raw", bufs=1))
         stage = ctx.enter_context(tc.tile_pool(name="stage", bufs=4))
         quant = ctx.enter_context(tc.tile_pool(name="quant", bufs=PASSES * GROUPS))
         ends = ctx.enter_context(tc.tile_pool(name="ends", bufs=GROUPS))
@@ -51,22 +51,11 @@ def tile_mix_glu48_tm_res_kernel(tc, x, w4_words, w4_scales, w8_words, w8_scales
             )
         raw_tiles = {}
 
-        def load_x(a, g):
-            t = raw.tile([P, PACK, GROUP], F32, name="rawx", align_bytes=64)
-            nc.sync.dma_start(out=t[:], in_=x_view[a][:, :, g * GROUP : (g + 1) * GROUP])
-            raw_tiles[a, g] = t[:]
-
-        load_x(0, 0)
-        def load_s8(q):
-            nc.scalar.dma_start(
-                out=s8[32 * q : 32 * q + 16, :].bitcast(I32),
-                in_=w8_scales[:, 4 * q : 4 * q + 4, :].bitcast(I32),
-            )
-
-        w8 = keep.tile([P, PASSES, N], U32, name="w8", align_bytes=64)
-        nc.sync.dma_start(out=w8[:].bitcast(I32), in_=w8_words.rearrange("a p n t -> p a (n t)").bitcast(I32))
-        w4 = keep.tile([P, PASSES, 2 * N], U8, name="w4", align_bytes=64)
-        nc.sync.dma_start(out=w4[:].bitcast(I32), in_=w4_words.rearrange("a p n -> p a n").bitcast(I32))
+        def load_x(a, g0, groups):
+            t = raw.tile([P, PACK, groups * GROUP], F32, name="raw%d_%d" % (a, g0), align_bytes=64)
+            nc.sync.dma_start(out=t[:], in_=x_view[a][:, :, g0 * GROUP : (g0 + groups) * GROUP])
+            for k in range(groups):
+                raw_tiles[a, g0 + k] = t[:, :, k * GROUP : (k + 1) * GROUP]
 
         r_tiles = {}
 
@@ -75,24 +64,29 @@ def tile_mix_glu48_tm_res_kernel(tc, x, w4_words, w4_scales, w8_words, w8_scales
             nc.sync.dma_start(out=t[:], in_=r_view[g])
             r_tiles[g] = t
 
-        load_x(1, 0)
+        load_x(0, 0, 3)
+        w4 = keep.tile([P, PASSES, 2 * N], U8, name="w4", align_bytes=64)
+        nc.sync.dma_start(out=w4[:].bitcast(I32), in_=w4_words.rearrange("a p n -> p a n").bitcast(I32))
+        w8 = keep.tile([P, PASSES, N], U32, name="w8", align_bytes=64)
+        nc.sync.dma_start(out=w8[:].bitcast(I32), in_=w8_words.rearrange("a p n t -> p a (n t)").bitcast(I32))
         for q in range(4):
-            load_s8(q)
+            nc.scalar.dma_start(
+                out=s8[32 * q : 32 * q + 16, :].bitcast(I32),
+                in_=w8_scales[:, 4 * q : 4 * q + 4, :].bitcast(I32),
+            )
         warm = keep.tile([P, 1], F32, name="warm")
         warm_out = keep.tile([P, 1], F32, name="warm_out")
         nc.vector.memset(warm[:], 0.0)
         nc.scalar.activation(out=warm_out[:], in_=warm[:], func=ACT.Silu)
-        for a in range(2, PASSES):
-            load_x(a, 0)
-        x0 = keep.tile([P, PACK, 2 * GROUP], F32, name="x0", align_bytes=64)
-        nc.sync.dma_start(out=x0[:], in_=x_view[0][:, :, GROUP:])
-        raw_tiles[0, 1] = x0[:, :, :GROUP]
-        raw_tiles[0, 2] = x0[:, :, GROUP:]
-        for a in range(1, PASSES):
-            load_x(a, 1)
+        load_x(1, 0, 1)
+        load_x(2, 0, 1)
+        load_x(3, 0, 1)
+        load_x(1, 1, 2)
+        load_x(2, 1, 1)
+        load_x(3, 1, 1)
         load_r(0)
-        for a in range(1, PASSES):
-            load_x(a, 2)
+        load_x(2, 2, 1)
+        load_x(3, 2, 1)
         load_r(1)
         load_r(2)
 
@@ -154,31 +148,30 @@ def tile_mix_glu48_tm_res_kernel(tc, x, w4_words, w4_scales, w8_words, w8_scales
         def store(g, i0, i1):
             nc.sync.dma_start(out=out_view[g][:, i0:i1, :], in_=y_tiles[g][:, i0:i1, :])
 
-        for a in range(PASSES):
+        prepare(0, 0)
+        multiply(0, 0)
+        prepare(0, 2)
+        prepare(0, 1)
+        for a in range(1, PASSES):
             prepare(a, 0)
             multiply(a, 0)
         for i in range(TILES):
             finish(0, i)
-        prepare(0, 1)
         multiply(0, 1)
-        prepare(0, 2)
         prepare(1, 1)
         multiply(1, 1)
         prepare(2, 1)
+        multiply(2, 1)
+        prepare(1, 2)
         prepare(3, 1)
-        for i in range(TILES):
-            multiply(2, 1, [i])
-            multiply(3, 1, [i])
+        multiply(3, 1)
         add(0, 0, 2)
         add(0, 2, 4)
         store(0, 0, 4)
-        finish(1, 0)
-        finish(1, 1)
-        prepare(1, 2)
-        finish(1, 2)
-        finish(1, 3)
-        multiply(0, 2)
-        multiply(1, 2)
+        for i in range(TILES):
+            finish(1, i)
+            multiply(0, 2, [i])
+            multiply(1, 2, [i])
         prepare(2, 2)
         prepare(3, 2)
         for i in range(TILES):

@@ -21,7 +21,7 @@ PASSES = K // (P * PACK)
 TILES = 4
 GROUP = P * TILES
 GROUPS = T // GROUP
-VECTOR_ROWS = (88, 64, 56)
+VECTOR_ROWS = 80
 
 
 def tile_mix_glu48_tm_res_kernel(tc, x, w4_words, w4_scales, w8_words, w8_scales, r, out):
@@ -69,24 +69,22 @@ def tile_mix_glu48_tm_res_kernel(tc, x, w4_words, w4_scales, w8_words, w8_scales
         nc.sync.dma_start(out=w4[:].bitcast(I32), in_=w4_words.rearrange("a p n -> p a n").bitcast(I32))
         w8 = keep.tile([P, PASSES, N], U32, name="w8", align_bytes=64)
         nc.sync.dma_start(out=w8[:].bitcast(I32), in_=w8_words.rearrange("a p n t -> p a (n t)").bitcast(I32))
+        warm = keep.tile([P, 1], F32, name="warm")
+        warm_out = keep.tile([P, 1], F32, name="warm_out")
+        nc.vector.memset(warm[:], 0.0)
+        nc.scalar.activation(out=warm_out[:], in_=warm[:], func=ACT.Silu)
         for q in range(4):
             nc.scalar.dma_start(
                 out=s8[32 * q : 32 * q + 16, :].bitcast(I32),
                 in_=w8_scales[:, 4 * q : 4 * q + 4, :].bitcast(I32),
             )
-        warm = keep.tile([P, 1], F32, name="warm")
-        warm_out = keep.tile([P, 1], F32, name="warm_out")
-        nc.vector.memset(warm[:], 0.0)
-        nc.scalar.activation(out=warm_out[:], in_=warm[:], func=ACT.Silu)
-        load_x(1, 0, 1)
-        load_x(2, 0, 1)
-        load_x(3, 0, 1)
-        load_x(1, 1, 2)
-        load_x(2, 1, 1)
-        load_x(3, 1, 1)
+        for a in range(1, PASSES):
+            load_x(a, 0, 1)
+        for a in range(1, PASSES):
+            load_x(a, 1, 1)
         load_r(0)
-        load_x(2, 2, 1)
-        load_x(3, 2, 1)
+        for a in range(1, PASSES):
+            load_x(a, 2, 1)
         load_r(1)
         load_r(2)
 
@@ -97,9 +95,8 @@ def tile_mix_glu48_tm_res_kernel(tc, x, w4_words, w4_scales, w8_words, w8_scales
             grouped = stage.tile([P, TILES, P, PACK], BF16, name="grouped", align_bytes=64)
             src = raw_tiles[a, g].rearrange("p j (m i) -> p m j i", i=TILES)
             dst = grouped[:].rearrange("p i m j -> p m j i")
-            mv = VECTOR_ROWS[g]
-            nc.scalar.copy(out=dst[:, mv:], in_=src[:, mv:])
-            nc.vector.tensor_copy(out=dst[:, :mv], in_=src[:, :mv])
+            nc.scalar.copy(out=dst[:, VECTOR_ROWS:], in_=src[:, VECTOR_ROWS:])
+            nc.vector.tensor_copy(out=dst[:, :VECTOR_ROWS], in_=src[:, :VECTOR_ROWS])
             c = quant.tile([P, GROUP], U32, name="codes", align_bytes=64)
             s = quant.tile([P, GROUP], U8, name="scales", align_bytes=64)
             nc.vector.quantize_mx(
@@ -150,37 +147,38 @@ def tile_mix_glu48_tm_res_kernel(tc, x, w4_words, w4_scales, w8_words, w8_scales
 
         prepare(0, 0)
         multiply(0, 0)
-        prepare(0, 2)
         prepare(0, 1)
+        prepare(0, 2)
         for a in range(1, PASSES):
             prepare(a, 0)
             multiply(a, 0)
+        prepare(1, 1)
         for i in range(TILES):
             finish(0, i)
         multiply(0, 1)
-        prepare(1, 1)
         multiply(1, 1)
         prepare(2, 1)
-        multiply(2, 1)
-        prepare(1, 2)
         prepare(3, 1)
-        multiply(3, 1)
+        for i in range(TILES):
+            multiply(2, 1, [i])
+            multiply(3, 1, [i])
         add(0, 0, 2)
         add(0, 2, 4)
         store(0, 0, 4)
-        for i in range(TILES):
+        finish(1, 0)
+        prepare(1, 2)
+        for i in range(1, TILES):
             finish(1, i)
-            multiply(0, 2, [i])
-            multiply(1, 2, [i])
+        multiply(0, 2)
+        multiply(1, 2)
         prepare(2, 2)
         prepare(3, 2)
         for i in range(TILES):
             multiply(2, 2, [i])
             multiply(3, 2, [i])
-        add(1, 0, 2)
-        store(1, 0, 2)
-        add(1, 2, 4)
-        store(1, 2, 4)
+        for i in range(0, TILES, 2):
+            add(1, i, i + 2)
+            store(1, i, i + 2)
         finish(2, 0)
         finish(2, 1)
         add(2, 0, 1)

from contextlib import ExitStack

import concourse.mybir as mybir

K, N, T = 2048, 512, 1536
FLOPS = 2 * 2 * K * N * T

F32 = mybir.dt.float32
BF16 = mybir.dt.bfloat16
I32 = mybir.dt.int32
U32 = mybir.dt.uint32
U8 = mybir.dt.uint8
FP8X4 = mybir.dt.float8_e4m3fn_x4
FP4X4 = mybir.dt.float4_e2m1fn_x4
ACT = mybir.ActivationFunctionType
ALU = mybir.AluOpType

P = 128
PACK = 4
PASSES = K // (P * PACK)
TILES = 4
GROUP = P * TILES
GROUPS = T // GROUP
VECTOR_ROWS = 80


def tile_mix_glu48_tm_res_kernel(tc, x, w4_words, w4_scales, w8_words, w8_scales, r, out):
    nc = tc.nc
    x_view = x.rearrange("(a p j) t -> a p j t", p=P, j=PACK)
    r_view = r.rearrange("(g m i) n -> g m i n", m=P, i=TILES)
    out_view = out.rearrange("(g m i) n -> g m i n", m=P, i=TILES)

    with ExitStack() as ctx:
        keep = ctx.enter_context(tc.tile_pool(name="keep", bufs=1))
        raw = ctx.enter_context(tc.tile_pool(name="raw", bufs=1))
        stage = ctx.enter_context(tc.tile_pool(name="stage", bufs=4))
        quant = ctx.enter_context(tc.tile_pool(name="quant", bufs=PASSES * GROUPS))
        ends = ctx.enter_context(tc.tile_pool(name="ends", bufs=GROUPS))
        psum = ctx.enter_context(tc.psum_pool(name="psum", bufs=1))
        ctx.enter_context(tc.manual_schedule())

        s4 = keep.tile([P, PASSES, N], U8, name="s4", align_bytes=64)
        s8 = keep.tile([P, N], U8, name="s8", align_bytes=64)
        nc.vector.memset(s4[:].rearrange("p a n -> p (a n)").bitcast(I32), 0)
        nc.vector.memset(s8[:].bitcast(I32), 0)

        for q in range(4):
            nc.scalar.dma_start(
                out=s4[32 * q : 32 * q + 4, :, :].bitcast(I32),
                in_=w4_scales.rearrange("a q n -> q a n")[4 * q : 4 * q + 4].bitcast(I32),
            )
        raw_tiles = {}

        def load_x(a, g0, groups):
            t = raw.tile([P, PACK, groups * GROUP], F32, name="raw%d_%d" % (a, g0), align_bytes=64)
            nc.sync.dma_start(out=t[:], in_=x_view[a][:, :, g0 * GROUP : (g0 + groups) * GROUP])
            for k in range(groups):
                raw_tiles[a, g0 + k] = t[:, :, k * GROUP : (k + 1) * GROUP]

        r_tiles = {}

        def load_r(g):
            t = ends.tile([P, TILES, N], F32, name="res")
            nc.sync.dma_start(out=t[:], in_=r_view[g])
            r_tiles[g] = t

        load_x(0, 0, 3)
        w4 = keep.tile([P, PASSES, 2 * N], U8, name="w4", align_bytes=64)
        nc.sync.dma_start(out=w4[:].bitcast(I32), in_=w4_words.rearrange("a p n -> p a n").bitcast(I32))
        w8 = keep.tile([P, PASSES, N], U32, name="w8", align_bytes=64)
        nc.sync.dma_start(out=w8[:].bitcast(I32), in_=w8_words.rearrange("a p n t -> p a (n t)").bitcast(I32))
        warm = keep.tile([P, 1], F32, name="warm")
        warm_out = keep.tile([P, 1], F32, name="warm_out")
        nc.vector.memset(warm[:], 0.0)
        nc.scalar.activation(out=warm_out[:], in_=warm[:], func=ACT.Silu)
        for q in range(4):
            nc.scalar.dma_start(
                out=s8[32 * q : 32 * q + 16, :].bitcast(I32),
                in_=w8_scales[:, 4 * q : 4 * q + 4, :].bitcast(I32),
            )
        for a in range(1, PASSES):
            load_x(a, 0, 1)
        for a in range(1, PASSES):
            load_x(a, 1, 1)
        load_r(0)
        for a in range(1, PASSES):
            load_x(a, 2, 1)
        load_r(1)
        load_r(2)

        codes = {}
        scales = {}

        def prepare(a, g):
            grouped = stage.tile([P, TILES, P, PACK], BF16, name="grouped", align_bytes=64)
            src = raw_tiles[a, g].rearrange("p j (m i) -> p m j i", i=TILES)
            dst = grouped[:].rearrange("p i m j -> p m j i")
            nc.scalar.copy(out=dst[:, VECTOR_ROWS:], in_=src[:, VECTOR_ROWS:])
            nc.vector.tensor_copy(out=dst[:, :VECTOR_ROWS], in_=src[:, :VECTOR_ROWS])
            c = quant.tile([P, GROUP], U32, name="codes", align_bytes=64)
            s = quant.tile([P, GROUP], U8, name="scales", align_bytes=64)
            nc.vector.quantize_mx(
                out=c[:].bitcast(FP8X4), scales=s[:], in_=grouped[:].rearrange("p i m j -> p (i m j)")
            )
            codes[a, g] = c
            scales[a, g] = s

        gate = {}
        up = {}

        def multiply(a, g, tiles=range(TILES)):
            for i in tiles:
                if a == 0:
                    gate[g, i] = psum.tile([P, N], F32, name="gate%d" % i)
                    up[g, i] = psum.tile([P, N], F32, name="up%d" % i)
                cols = slice(i * P, (i + 1) * P)
                lhs = codes[a, g][:, cols].bitcast(FP8X4)
                lhs_scale = scales[a, g][:, cols]
                flags = dict(start=(a == 0), stop=(a == PASSES - 1))
                nc.tensor.matmul_mx(
                    out=gate[g, i][:], lhsT=lhs, lhsT_scale=lhs_scale,
                    rhs=w4[:, a, :].bitcast(FP4X4), rhs_scale=s4[:, a, :], **flags,
                )
                w8_scale = s8[4 * a :, :]
                nc.tensor.matmul_mx(
                    out=up[g, i][:], lhsT=lhs, lhsT_scale=lhs_scale,
                    rhs=w8[:, a, :].bitcast(FP8X4), rhs_scale=w8_scale, **flags,
                )

        y_tiles = {}

        def finish(g, i):
            if i == 0:
                y_tiles[g] = ends.tile([P, TILES, N], F32, name="y")
            s = stage.tile([P, N], F32, name="silu")
            nc.scalar.activation(out=s[:], in_=gate[g, i][:], func=ACT.Silu)
            nc.vector.tensor_tensor(out=y_tiles[g][:, i, :], in0=s[:], in1=up[g, i][:], op=ALU.mult)

        def add(g, i0, i1):
            y = y_tiles[g]
            nc.vector.tensor_tensor(
                out=y[:, i0:i1, :], in0=y[:, i0:i1, :], in1=r_tiles[g][:, i0:i1, :], op=ALU.add
            )

        def store(g, i0, i1):
            nc.sync.dma_start(out=out_view[g][:, i0:i1, :], in_=y_tiles[g][:, i0:i1, :])

        prepare(0, 0)
        multiply(0, 0)
        prepare(0, 1)
        prepare(0, 2)
        for a in range(1, PASSES):
            prepare(a, 0)
            multiply(a, 0)
        prepare(1, 1)
        for i in range(TILES):
            finish(0, i)
        multiply(0, 1)
        multiply(1, 1)
        prepare(2, 1)
        prepare(3, 1)
        for i in range(TILES):
            multiply(2, 1, [i])
            multiply(3, 1, [i])
        add(0, 0, 2)
        add(0, 2, 4)
        store(0, 0, 4)
        finish(1, 0)
        prepare(1, 2)
        for i in range(1, TILES):
            finish(1, i)
        multiply(0, 2)
        multiply(1, 2)
        prepare(2, 2)
        prepare(3, 2)
        for i in range(TILES):
            multiply(2, 2, [i])
            multiply(3, 2, [i])
        for i in range(0, TILES, 2):
            add(1, i, i + 2)
            store(1, i, i + 2)
        finish(2, 0)
        finish(2, 1)
        add(2, 0, 1)
        finish(2, 2)
        add(2, 1, 2)
        store(2, 0, 2)
        finish(2, 3)
        add(2, 2, 3)
        add(2, 3, 4)
        store(2, 2, 4)
